import numpy as np
import ml_dtypes


def mxq(x, axis, fmt="e4m3"):
    dtype, down = {"e4m3": (ml_dtypes.float8_e4m3fn, 7), "e5m2": (ml_dtypes.float8_e5m2, 14)}[fmt]
    v = np.moveaxis(np.asarray(x, np.float32).astype(ml_dtypes.bfloat16).astype(np.float64), axis, -1)
    blocks = v.reshape(v.shape[:-1] + (-1, 32))
    amax = np.abs(blocks).max(-1, keepdims=True)
    byte = np.maximum(np.where(amax > 0, np.frexp(amax)[1] - 1 + 127, 0) - down, 1)
    scale = np.exp2(byte - 127.0)
    codes = (blocks / scale).astype(np.float32).astype(dtype).astype(np.float64)
    return np.moveaxis((codes * scale).reshape(v.shape), -1, axis)


WIDE = False


def mx_kscale(k):
    if not WIDE:
        return np.ones(k)
    levels = np.array([10, -10, 5, -5, 0])
    if k % 512:
        return np.exp2(np.random.permutation(np.resize(levels, k // 32))).repeat(32)
    a = np.empty((k // 512, 16))
    for p in range(k // 512):
        a[p, :8] = np.random.permutation(np.resize(levels, 8))
        for g in range(8):
            far = levels[np.abs(levels - a[p, g]) >= 10]
            a[p, g + 8] = far[np.random.randint(len(far))]
    return np.exp2(a.ravel()).repeat(32)


def f64(x):
    return np.asarray(x).astype(np.float64)


def striped(idx):
    return np.tile(idx.reshape(-1, 16).T, (8, 1)).astype(np.uint16)


def unstriped(offs):
    return offs[:16].T.reshape(-1).astype(np.int64)


def pack_weight(w):
    k, n = w.shape
    w = f64(np.asarray(w, np.float32).astype(ml_dtypes.bfloat16)).reshape(k // 32, 32, n)
    amax = np.abs(w).max(1)
    byte = np.clip(np.where(amax > 0, np.frexp(amax)[1] - 1 + 127 - 7, 1), 1, 254)
    scaled = (w * np.exp2(127.0 - byte)[:, None, :]).reshape(k, n).astype(np.float32)
    words = np.ascontiguousarray(scaled.reshape(k // 512, 128, 4, n).transpose(0, 1, 3, 2)).astype(ml_dtypes.float8_e4m3fn).view(np.uint8)
    return words, np.ascontiguousarray(byte.astype(np.uint8).reshape(k // 512, 16, n))


def unpack_weight(words, scales):
    g, p, n, _ = words.shape
    vals = np.ascontiguousarray(words).view(ml_dtypes.float8_e4m3fn).astype(np.float64) * np.repeat(np.exp2(scales.astype(np.float64) - 127.0), 8, axis=1)[..., None]
    return vals.transpose(0, 1, 3, 2).reshape(g * 512, n)


E2M1 = np.array([0.0, 0.5, 1.0, 1.5, 2.0, 3.0, 4.0, 6.0, -0.0, -0.5, -1.0, -1.5, -2.0, -3.0, -4.0, -6.0])


def pack_fp4(w):
    k, n = w.shape
    w = f64(np.asarray(w, np.float32).astype(ml_dtypes.bfloat16)).reshape(k // 32, 32, n)
    amax = np.abs(w).max(1)
    mant, ex = np.frexp(amax / 6.0)
    byte = np.clip(np.where(amax > 0, np.where(mant > 0.5, ex, ex - 1) + 127, 1), 1, 254)
    scaled = (w * np.exp2(127.0 - byte)[:, None, :]).reshape(k, n).astype(np.float32)
    c = np.ascontiguousarray(scaled.reshape(k // 512, 128, 4, n).transpose(0, 1, 3, 2)).astype(ml_dtypes.float4_e2m1fn).view(np.uint8) & 0xF
    words = (c[..., 0::2] | (c[..., 1::2] << 4)).reshape(k // 512, 128, 2 * n)
    return np.ascontiguousarray(words), np.ascontiguousarray(byte.astype(np.uint8).reshape(k // 512, 16, n))


def unpack_fp4(words, scales):
    g, _, n = scales.shape
    words = np.ascontiguousarray(words).reshape(g, 128, n, 2)
    nib = np.empty((g, 128, n, 4), np.uint8)
    nib[..., 0::2] = words & 0xF
    nib[..., 1::2] = words >> 4
    vals = E2M1[nib] * np.repeat(np.exp2(scales.astype(np.float64) - 127.0), 8, axis=1)[..., None]
    return vals.transpose(0, 1, 3, 2).reshape(g * 512, n)


K, T, S, D, N, H = 512, 2048, 1024, 2, 256, 512


def setup_inputs():
    n = np.random.standard_normal
    s = mx_kscale(K)[:, None]
    u = mx_kscale(H)
    packed_xT = pack_weight(n((K, T)) * s)
    packed_w1 = pack_fp4(n((K, H)) / np.sqrt(K) / s)
    packed_w2 = pack_fp4(n((K, H)) / np.sqrt(K) / s)
    packed_w3 = pack_fp4(n((H, N)) / np.sqrt(H) / u[:, None])
    return {
        "x_words": packed_xT[0],
        "x_scales": packed_xT[1],
        "w1_words": packed_w1[0],
        "w1_scales": packed_w1[1],
        "w2_words": packed_w2[0],
        "w2_scales": packed_w2[1],
        "unit": (np.random.uniform(0.6, 1.4, (H, 1)) * u[:, None]).astype(np.float32),
        "w3_words": packed_w3[0],
        "w3_scales": packed_w3[1],
        "offs": striped(np.random.permutation(T)[:S]),
        "ovl": striped(np.random.permutation(S)),
    }


def reference(x_words, x_scales, w1_words, w1_scales, w2_words, w2_scales, unit, w3_words, w3_scales, offs, ovl):
    xq = unpack_weight(x_words, x_scales)[:, unstriped(offs)]
    mt = unpack_fp4(w1_words, w1_scales).T @ xq
    tmem = np.log(np.exp(mt) + 1.0)
    ft = unpack_fp4(w2_words, w2_scales).T @ xq
    tflop = np.log(np.exp(ft) + 1.0)
    roof = np.maximum(tmem, tflop)
    tmo = tmem[:, unstriped(ovl)]
    hidd = np.minimum(tmo, tflop)
    exec_ = roof + 0.3 * (tmem + tflop - roof) - (0.6 * hidd)
    wave = exec_.reshape(len(exec_), -1, D).max(axis=2)
    hid = f64(unit) * ((exec_ / (np.repeat(wave, D, axis=1) + 0.3)) * tflop)
    return unpack_fp4(w3_words, w3_scales).T @ mxq(hid, 0, "e4m3")

@@ -1,0 +1,221 @@
+from contextlib import ExitStack
+
+import concourse.mybir as mybir
+
+K, T, S, H, N = 512, 2048, 1024, 512, 256
+FLOPS = 2 * K * H * S * 2 + 2 * H * N * S
+
+F32 = mybir.dt.float32
+BF16 = mybir.dt.bfloat16
+I32 = mybir.dt.int32
+U32 = mybir.dt.uint32
+U16 = mybir.dt.uint16
+U8 = mybir.dt.uint8
+FP8X4 = mybir.dt.float8_e4m3fn_x4
+FP4X4 = mybir.dt.float4_e2m1fn_x4
+ALU = mybir.AluOpType
+ACT = mybir.ActivationFunctionType
+
+P = 128
+PACK = 4
+BANK = 512
+HALVES = S // BANK
+LIST_ROWS = 16
+TINY = 2.0**-60
+ROUNDS = [(0,), (1, 2), (3,)]
+PIECE = 256
+
+
+def tile_picked_ygpusch_rel_p_kernel(
+    tc, x_words, x_scales, w1_words, w1_scales, w2_words, w2_scales, unit, w3_words, w3_scales, offs, ovl, out
+):
+    nc = tc.nc
+    with ExitStack() as ctx:
+        keep = ctx.enter_context(tc.tile_pool(name="keep", bufs=1))
+        work = ctx.enter_context(tc.tile_pool(name="work", bufs=2))
+        psum = ctx.enter_context(tc.psum_pool(name="psum", bufs=8))
+
+        def load_scale_rows(queue, plane, rows):
+            for q in range(4):
+                queue.dma_start(out=plane[32 * q : 32 * q + 4, :].bitcast(I32), in_=rows[0, 4 * q : 4 * q + 4, :].bitcast(I32))
+
+        def half(h):
+            return slice(h * BANK, (h + 1) * BANK)
+
+        offs_t = keep.tile([P, S // LIST_ROWS], U16, name="offs_t")
+        ovl_t = keep.tile([P, S // LIST_ROWS], U16, name="ovl_t")
+        xw = keep.tile([P, T], U32, name="xw", align_bytes=64)
+        xs = keep.tile([P, T], U8, name="xs", align_bytes=64)
+        raw_w = [keep.tile([P, 2 * H], U8, name=f"raw_w{i}", align_bytes=64) for i in range(2)]
+        raw_s = [keep.tile([P, H], U8, name=f"raw_s{i}", align_bytes=64) for i in range(2)]
+        w3w = keep.tile([P, 2 * N], U8, name="w3w", align_bytes=64)
+        w3s = keep.tile([P, N], U8, name="w3s", align_bytes=64)
+        unit_t = keep.tile([P, PACK], F32, name="unit_t")
+
+        nc.vector.memset(xs[:].bitcast(I32), 0)
+        for plane in (raw_s[0], raw_s[1], w3s):
+            nc.vector.memset(plane[:].bitcast(I32), 0)
+
+        nc.sync.dma_start(out=offs_t[:], in_=offs)
+        nc.sync.dma_start(out=raw_w[0][:].bitcast(I32), in_=w1_words[0].bitcast(I32))
+        nc.sync.dma_start(out=raw_w[1][:].bitcast(I32), in_=w2_words[0].bitcast(I32))
+        load_scale_rows(nc.sync, xs, x_scales)
+        nc.sync.dma_start(out=xw[:].bitcast(I32), in_=x_words[0].rearrange("p n t -> p (n t)").bitcast(I32))
+        load_scale_rows(nc.sync, raw_s[0], w1_scales)
+        load_scale_rows(nc.sync, raw_s[1], w2_scales)
+        nc.sync.dma_start(out=ovl_t[:], in_=ovl)
+        nc.sync.dma_start(out=unit_t[:], in_=unit.rearrange("(p t) o -> p (t o)", t=PACK))
+        nc.sync.dma_start(out=w3w[:].bitcast(I32), in_=w3_words[0].bitcast(I32))
+        load_scale_rows(nc.sync, w3s, w3_scales)
+
+        dealt_w = [[keep.tile([P, 2 * P], U8, name=f"dealt_w{i}_{t}", align_bytes=64) for t in range(PACK)] for i in range(2)]
+        dealt_s = [[keep.tile([P, P], U8, name=f"dealt_s{i}_{t}", align_bytes=64) for t in range(PACK)] for i in range(2)]
+
+        def deal(t):
+            for i in range(2):
+                nc.vector.tensor_copy(
+                    out=dealt_w[i][t][:].rearrange("p (m e) -> p m e", e=2),
+                    in_=raw_w[i][:].rearrange("p (m t e) -> p t m e", t=PACK, e=2)[:, t],
+                )
+                nc.vector.tensor_copy(out=dealt_s[i][t][:], in_=raw_s[i][:].rearrange("p (m t) -> p t m", t=PACK)[:, t])
+
+        def entries(lst, h):
+            cols = BANK // LIST_ROWS
+            return lst[:, h * cols : (h + 1) * cols]
+
+        gw = [keep.tile([P, BANK], U32, name=f"gw{h}", align_bytes=64) for h in range(HALVES)]
+        gs = [keep.tile([P, BANK], U8, name=f"gs{h}", align_bytes=64) for h in range(HALVES)]
+        for h in range(HALVES):
+            nc.vector.tensor_copy(out=gs[h][:], in_=xs[:].indirect(entries(offs_t, h)))
+            nc.vector.tensor_copy(out=gw[h][:], in_=xw[:].indirect(entries(offs_t, h)))
+            if h == 0:
+                deal(0)
+        for t in range(1, PACK):
+            deal(t)
+
+        tflop = keep.tile([P, PACK, S], F32, name="tflop")
+        execs = keep.tile([P, PACK, S], F32, name="execs")
+        wave = keep.tile([P, PACK, S // 2], F32, name="wave")
+        lnwave = keep.tile([P, PACK, S // 2], F32, name="lnwave")
+
+        for tiles in ROUNDS:
+            jobs = [(t, i, h) for t in tiles for i in range(2) for h in range(HALVES)]
+            nb = len(jobs)
+            share = BANK // nb
+            row = share + BANK
+            sig = work.tile([P, nb * row], F32, name="sig")
+            lns = sig
+
+            def place(tile, k):
+                if k < nb - 1:
+                    return tile[:, k * row + share : (k + 1) * row]
+                return tile[:].rearrange("p (k r) -> p k r", r=row)[:, :, 0:share]
+
+            def shaped(ap, k):
+                return ap if k < nb - 1 else ap.rearrange("p (k r) -> p k r", r=share)
+
+            banks = []
+            for k, (t, i, h) in enumerate(jobs):
+                bank = psum.tile([P, BANK], F32, name="bank")
+                banks.append(bank)
+                nc.tensor.matmul_mx(
+                    out=bank[:],
+                    lhsT=dealt_w[i][t][:].bitcast(FP4X4),
+                    lhsT_scale=dealt_s[i][t][:],
+                    rhs=gw[h][:].bitcast(FP8X4),
+                    rhs_scale=gs[h][:],
+                    start=True,
+                    stop=True,
+                )
+                nc.scalar.activation(out=place(sig, k), in_=shaped(bank[:], k), func=ACT.Sigmoid, scale=-1.0)
+
+            for t in tiles:
+                tmem = work.tile([P, S], F32, name="tmem")
+                tmo = work.tile([P, S], F32, name="tmo")
+                roof = work.tile([P, S], F32, name="roof")
+                part = work.tile([P, S], F32, name="part")
+                hidd = work.tile([P, S], F32, name="hidd")
+                rest = work.tile([P, S], F32, name="rest")
+                mine = [k for k, job in enumerate(jobs) if job[0] == t]
+                for k in mine:
+                    if k < nb - 1:
+                        cols = slice(k * row, (k + 1) * row + (share if k == nb - 2 else 0))
+                        nc.scalar.activation(out=lns[:, cols], in_=sig[:, cols], func=ACT.Ln, bias=TINY)
+                for k in mine:
+                    i, h = jobs[k][1:]
+                    target = tmem[:, half(h)] if i == 0 else tflop[:, t, half(h)]
+                    nc.vector.scalar_tensor_tensor(
+                        out=shaped(target, k), in0=place(lns, k), scalar=-1.0, in1=shaped(banks[k][:], k), op0=ALU.mult, op1=ALU.max
+                    )
+                for h in range(HALVES):
+                    fetched = tmem[:].indirect(entries(ovl_t, h))
+                    if t == 0:
+                        nc.vector.tensor_copy(out=tmo[:, half(h)], in_=fetched)
+                    else:
+                        nc.scalar.activation(out=tmo[:, half(h)], in_=fetched, func=ACT.Copy)
+                for h in range(HALVES):
+                    nc.vector.tensor_tensor(out=roof[:, half(h)], in0=tmem[:, half(h)], in1=tflop[:, t, half(h)], op=ALU.max)
+                for h in range(HALVES):
+                    nc.vector.scalar_tensor_tensor(
+                        out=part[:, half(h)], in0=roof[:, half(h)], scalar=0.7 / 0.3, in1=tmem[:, half(h)], op0=ALU.mult, op1=ALU.add
+                    )
+                for h in range(HALVES):
+                    nc.vector.tensor_tensor(out=hidd[:, half(h)], in0=tmo[:, half(h)], in1=tflop[:, t, half(h)], op=ALU.min)
+                for h in range(HALVES):
+                    nc.vector.scalar_tensor_tensor(
+                        out=rest[:, half(h)], in0=hidd[:, half(h)], scalar=-2.0, in1=tflop[:, t, half(h)], op0=ALU.mult, op1=ALU.add
+                    )
+                for h in range(HALVES):
+                    nc.vector.tensor_tensor(out=execs[:, t, half(h)], in0=part[:, half(h)], in1=rest[:, half(h)], op=ALU.add)
+                for h in range(HALVES):
+                    pairs = execs[:, t, half(h)].rearrange("p (v d) -> p v d", d=2)
+                    nc.vector.tensor_tensor(
+                        out=wave[:, t, h * BANK // 2 : (h + 1) * BANK // 2], in0=pairs[:, :, 0], in1=pairs[:, :, 1], op=ALU.max
+                    )
+
+        nc.scalar.activation(out=lnwave[:, 0 : PACK - 1, :], in_=wave[:, 0 : PACK - 1, :], func=ACT.Ln, bias=TINY)
+        nc.scalar.activation(out=lnwave[:, PACK - 1, :], in_=wave[:, PACK - 1, :], func=ACT.Ln, bias=TINY)
+
+        prod = keep.tile([P, PACK, S], F32, name="prod")
+        for t in range(PACK):
+            nc.vector.scalar_tensor_tensor(
+                out=prod[:, t, :], in0=execs[:, t, :], scalar=unit_t[:, t : t + 1], in1=tflop[:, t, :], op0=ALU.mult, op1=ALU.mult
+            )
+
+        out_view = out.rearrange("(a p) n -> p a n", p=P)
+        pieces = S // PIECE
+        waves = PIECE // 2
+        hids = []
+        for c in range(pieces):
+            rec = keep.tile([P, waves, PACK], F32, name=f"rec{c}")
+            nc.scalar.activation(
+                out=rec[:], in_=lnwave[:, :, c * waves : (c + 1) * waves].rearrange("p t v -> p v t"), func=ACT.Sigmoid, scale=-1.0
+            )
+            hid = keep.tile([P, PIECE * PACK], BF16, name=f"hid{c}", align_bytes=64)
+            hids.append(hid)
+            nc.vector.tensor_tensor(
+                out=hid[:].rearrange("p (v d t) -> p v t d", d=2, t=PACK),
+                in0=prod[:, :, c * PIECE : (c + 1) * PIECE].rearrange("p t (v d) -> p v t d", d=2),
+                in1=rec[:].unsqueeze(3).to_broadcast([P, waves, PACK, 2]),
+                op=ALU.mult,
+            )
+            for done in ([c - 1] if c > 0 else []) + ([c] if c == pieces - 1 else []):
+                codes = keep.tile([P, PIECE], U32, name=f"codes{done}", align_bytes=64)
+                scales = keep.tile([P, PIECE], U8, name=f"scales{done}", align_bytes=64)
+                nc.vector.quantize_mx(out=codes[:].bitcast(FP8X4), scales=scales[:], in_=hids[done][:])
+                bank = psum.tile([P, BANK], F32, name="bank")
+                for a in range(N // P):
+                    nc.tensor.matmul_mx(
+                        out=bank[:, a * PIECE : (a + 1) * PIECE],
+                        lhsT=w3w[:, 2 * a * P : 2 * (a + 1) * P].bitcast(FP4X4),
+                        lhsT_scale=w3s[:, a * P : (a + 1) * P],
+                        rhs=codes[:].bitcast(FP8X4),
+                        rhs_scale=scales[:],
+                        start=True,
+                        stop=True,
+                    )
+                result = keep.tile([P, BANK], F32, name=f"result{done}")
+                nc.scalar.copy(out=result[:], in_=bank[:])
+                nc.sync.dma_start(
+                    out=out_view[:, :, done * PIECE : (done + 1) * PIECE], in_=result[:].rearrange("p (a n) -> p a n", n=PIECE)
+                )

@@ -22,8 +22,8 @@ BANK = 512
 HALVES = S // BANK
 LIST_ROWS = 16
 TINY = 2.0**-60
-ROUNDS = [(0,), (1, 2), (3,)]
-PIECE = 256
+ROUNDS = [(0, 1), (2, 3)]
+PIECES = [256, 256, 256, 128, 128]
 
 
 def tile_picked_ygpusch_rel_p_kernel(
@@ -35,8 +35,8 @@ def tile_picked_ygpusch_rel_p_kernel(
         work = ctx.enter_context(tc.tile_pool(name="work", bufs=2))
         psum = ctx.enter_context(tc.psum_pool(name="psum", bufs=8))
 
-        def load_scale_rows(queue, plane, rows):
-            for q in range(4):
+        def load_scale_rows(queues, plane, rows):
+            for q, queue in enumerate(queues):
                 queue.dma_start(out=plane[32 * q : 32 * q + 4, :].bitcast(I32), in_=rows[0, 4 * q : 4 * q + 4, :].bitcast(I32))
 
         def half(h):
@@ -48,57 +48,71 @@ def tile_picked_ygpusch_rel_p_kernel(
         xs = keep.tile([P, T], U8, name="xs", align_bytes=64)
         raw_w = [keep.tile([P, 2 * H], U8, name=f"raw_w{i}", align_bytes=64) for i in range(2)]
         raw_s = [keep.tile([P, H], U8, name=f"raw_s{i}", align_bytes=64) for i in range(2)]
-        w3w = keep.tile([P, 2 * N], U8, name="w3w", align_bytes=64)
-        w3s = keep.tile([P, N], U8, name="w3s", align_bytes=64)
-        unit_t = keep.tile([P, PACK], F32, name="unit_t")
 
-        nc.vector.memset(xs[:].bitcast(I32), 0)
-        for plane in (raw_s[0], raw_s[1], w3s):
+        for plane in (xs, raw_s[0], raw_s[1]):
             nc.vector.memset(plane[:].bitcast(I32), 0)
 
-        nc.sync.dma_start(out=offs_t[:], in_=offs)
         nc.sync.dma_start(out=raw_w[0][:].bitcast(I32), in_=w1_words[0].bitcast(I32))
-        nc.sync.dma_start(out=raw_w[1][:].bitcast(I32), in_=w2_words[0].bitcast(I32))
-        load_scale_rows(nc.sync, xs, x_scales)
-        nc.sync.dma_start(out=xw[:].bitcast(I32), in_=x_words[0].rearrange("p n t -> p (n t)").bitcast(I32))
-        load_scale_rows(nc.sync, raw_s[0], w1_scales)
-        load_scale_rows(nc.sync, raw_s[1], w2_scales)
+        nc.sync.dma_start(out=offs_t[:], in_=offs)
         nc.sync.dma_start(out=ovl_t[:], in_=ovl)
-        nc.sync.dma_start(out=unit_t[:], in_=unit.rearrange("(p t) o -> p (t o)", t=PACK))
-        nc.sync.dma_start(out=w3w[:].bitcast(I32), in_=w3_words[0].bitcast(I32))
-        load_scale_rows(nc.sync, w3s, w3_scales)
+        load_scale_rows([nc.sync, nc.sync, nc.scalar, nc.scalar], xs, x_scales)
+        nc.sync.dma_start(out=xw[:].bitcast(I32), in_=x_words[0].rearrange("p n t -> p (n t)").bitcast(I32))
+        nc.gpsimd.dma_start(out=raw_w[1][:].bitcast(I32), in_=w2_words[0].bitcast(I32))
+        load_scale_rows([nc.sync] * 4, raw_s[0], w1_scales)
+        load_scale_rows([nc.sync] * 4, raw_s[1], w2_scales)
 
-        dealt_w = [[keep.tile([P, 2 * P], U8, name=f"dealt_w{i}_{t}", align_bytes=64) for t in range(PACK)] for i in range(2)]
-        dealt_s = [[keep.tile([P, P], U8, name=f"dealt_s{i}_{t}", align_bytes=64) for t in range(PACK)] for i in range(2)]
-
-        def deal(t):
+        def deal_words(tiles):
+            words = [keep.tile([P, len(tiles), 2 * P], U8, name=f"dealt_w{i}", align_bytes=64) for i in range(2)]
             for i in range(2):
                 nc.vector.tensor_copy(
-                    out=dealt_w[i][t][:].rearrange("p (m e) -> p m e", e=2),
-                    in_=raw_w[i][:].rearrange("p (m t e) -> p t m e", t=PACK, e=2)[:, t],
+                    out=words[i][:].rearrange("p t (m e) -> p t m e", e=2),
+                    in_=raw_w[i][:].rearrange("p (m t e) -> p t m e", t=PACK, e=2)[:, tiles[0] : tiles[-1] + 1],
                 )
-                nc.vector.tensor_copy(out=dealt_s[i][t][:], in_=raw_s[i][:].rearrange("p (m t) -> p t m", t=PACK)[:, t])
+            return words
+
+        dealt_w = deal_words(ROUNDS[0])
+        dealt_s = [keep.tile([P, PACK, P], U8, name=f"dealt_s{i}", align_bytes=64) for i in range(2)]
+        for i in range(2):
+            nc.vector.tensor_copy(out=dealt_s[i][:], in_=raw_s[i][:].rearrange("p (m t) -> p t m", t=PACK))
+        w3s = raw_s[1][:, 0:N]
+        load_scale_rows([nc.sync] * 4, w3s, w3_scales)
 
         def entries(lst, h):
             cols = BANK // LIST_ROWS
             return lst[:, h * cols : (h + 1) * cols]
 
-        gw = [keep.tile([P, BANK], U32, name=f"gw{h}", align_bytes=64) for h in range(HALVES)]
+        gw = [keep.tile([P, BANK], U32, name=name, align_bytes=64) for name in ("gw0", "raw_s0")]
         gs = [keep.tile([P, BANK], U8, name=f"gs{h}", align_bytes=64) for h in range(HALVES)]
         for h in range(HALVES):
             nc.vector.tensor_copy(out=gs[h][:], in_=xs[:].indirect(entries(offs_t, h)))
             nc.vector.tensor_copy(out=gw[h][:], in_=xw[:].indirect(entries(offs_t, h)))
-            if h == 0:
-                deal(0)
-        for t in range(1, PACK):
-            deal(t)
 
         tflop = keep.tile([P, PACK, S], F32, name="tflop")
         execs = keep.tile([P, PACK, S], F32, name="execs")
         wave = keep.tile([P, PACK, S // 2], F32, name="wave")
         lnwave = keep.tile([P, PACK, S // 2], F32, name="lnwave")
 
+        spans = [half(0), half(1)]
+
+        unit_t = keep.tile([P, PACK], F32, name="xs", align_bytes=64)
+        nc.sync.dma_start(out=unit_t[:], in_=unit.rearrange("(p t) o -> p (t o)", t=PACK))
+        prod = keep.tile([P, PACK, S], F32, name="prod")
+
+        def weigh(t):
+            nc.vector.scalar_tensor_tensor(
+                out=prod[:, t, :], in0=execs[:, t, :], scalar=unit_t[:, t : t + 1], in1=tflop[:, t, :], op0=ALU.mult, op1=ALU.mult
+            )
+
+        def pair_max(t):
+            for cols in spans:
+                pairs = execs[:, t, cols].rearrange("p (v d) -> p v d", d=2)
+                nc.vector.tensor_tensor(out=wave[:, t, cols.start // 2 : cols.stop // 2], in0=pairs[:, :, 0], in1=pairs[:, :, 1], op=ALU.max)
+
         for tiles in ROUNDS:
+            if tiles != ROUNDS[0]:
+                dealt_w = deal_words(tiles)
+                w3w = raw_w[0][:, 0 : 2 * N]
+                nc.sync.dma_start(out=w3w.bitcast(I32), in_=w3_words[0].bitcast(I32))
             jobs = [(t, i, h) for t in tiles for i in range(2) for h in range(HALVES)]
             nb = len(jobs)
             share = BANK // nb
@@ -114,14 +128,15 @@ def tile_picked_ygpusch_rel_p_kernel(
             def shaped(ap, k):
                 return ap if k < nb - 1 else ap.rearrange("p (k r) -> p k r", r=share)
 
-            banks = []
-            for k, (t, i, h) in enumerate(jobs):
+            banks = {}
+            for k in sorted(range(nb), key=lambda k: (jobs[k][2], jobs[k][1]) if tiles == ROUNDS[0] else k):
+                t, i, h = jobs[k]
                 bank = psum.tile([P, BANK], F32, name="bank")
-                banks.append(bank)
+                banks[k] = bank
                 nc.tensor.matmul_mx(
                     out=bank[:],
-                    lhsT=dealt_w[i][t][:].bitcast(FP4X4),
-                    lhsT_scale=dealt_s[i][t][:],
+                    lhsT=dealt_w[i][:, t - tiles[0], :].bitcast(FP4X4),
+                    lhsT_scale=dealt_s[i][:, t, :],
                     rhs=gw[h][:].bitcast(FP8X4),
                     rhs_scale=gs[h][:],
                     start=True,
@@ -148,74 +163,70 @@ def tile_picked_ygpusch_rel_p_kernel(
                         out=shaped(target, k), in0=place(lns, k), scalar=-1.0, in1=shaped(banks[k][:], k), op0=ALU.mult, op1=ALU.max
                     )
                 for h in range(HALVES):
-                    fetched = tmem[:].indirect(entries(ovl_t, h))
-                    if t == 0:
-                        nc.vector.tensor_copy(out=tmo[:, half(h)], in_=fetched)
-                    else:
-                        nc.scalar.activation(out=tmo[:, half(h)], in_=fetched, func=ACT.Copy)
-                for h in range(HALVES):
-                    nc.vector.tensor_tensor(out=roof[:, half(h)], in0=tmem[:, half(h)], in1=tflop[:, t, half(h)], op=ALU.max)
-                for h in range(HALVES):
+                    nc.scalar.activation(out=tmo[:, half(h)], in_=tmem[:].indirect(entries(ovl_t, h)), func=ACT.Copy)
+                if t > 0:
+                    pair_max(t - 1)
+                for cols in spans:
+                    nc.vector.tensor_tensor(out=roof[:, cols], in0=tmem[:, cols], in1=tflop[:, t, cols], op=ALU.max)
+                for cols in spans:
                     nc.vector.scalar_tensor_tensor(
-                        out=part[:, half(h)], in0=roof[:, half(h)], scalar=0.7 / 0.3, in1=tmem[:, half(h)], op0=ALU.mult, op1=ALU.add
+                        out=part[:, cols], in0=roof[:, cols], scalar=0.7 / 0.3, in1=tmem[:, cols], op0=ALU.mult, op1=ALU.add
                     )
-                for h in range(HALVES):
-                    nc.vector.tensor_tensor(out=hidd[:, half(h)], in0=tmo[:, half(h)], in1=tflop[:, t, half(h)], op=ALU.min)
-                for h in range(HALVES):
+                for cols in spans:
+                    nc.vector.tensor_tensor(out=hidd[:, cols], in0=tmo[:, cols], in1=tflop[:, t, cols], op=ALU.min)
+                for cols in spans:
                     nc.vector.scalar_tensor_tensor(
-                        out=rest[:, half(h)], in0=hidd[:, half(h)], scalar=-2.0, in1=tflop[:, t, half(h)], op0=ALU.mult, op1=ALU.add
+                        out=rest[:, cols], in0=hidd[:, cols], scalar=-2.0, in1=tflop[:, t, cols], op0=ALU.mult, op1=ALU.add
                     )
-                for h in range(HALVES):
-                    nc.vector.tensor_tensor(out=execs[:, t, half(h)], in0=part[:, half(h)], in1=rest[:, half(h)], op=ALU.add)
-                for h in range(HALVES):
-                    pairs = execs[:, t, half(h)].rearrange("p (v d) -> p v d", d=2)
-                    nc.vector.tensor_tensor(
-                        out=wave[:, t, h * BANK // 2 : (h + 1) * BANK // 2], in0=pairs[:, :, 0], in1=pairs[:, :, 1], op=ALU.max
-                    )
+                adder = nc.vector
+                for cols in [half(0), half(1)]:
+                    adder.tensor_tensor(out=execs[:, t, cols], in0=part[:, cols], in1=rest[:, cols], op=ALU.add)
+        pair_max(PACK - 1)
 
         nc.scalar.activation(out=lnwave[:, 0 : PACK - 1, :], in_=wave[:, 0 : PACK - 1, :], func=ACT.Ln, bias=TINY)
         nc.scalar.activation(out=lnwave[:, PACK - 1, :], in_=wave[:, PACK - 1, :], func=ACT.Ln, bias=TINY)
 
-        prod = keep.tile([P, PACK, S], F32, name="prod")
-        for t in range(PACK):
-            nc.vector.scalar_tensor_tensor(
-                out=prod[:, t, :], in0=execs[:, t, :], scalar=unit_t[:, t : t + 1], in1=tflop[:, t, :], op0=ALU.mult, op1=ALU.mult
-            )
+        for t in range(0, PACK):
+            weigh(t)
 
         out_view = out.rearrange("(a p) n -> p a n", p=P)
-        pieces = S // PIECE
-        waves = PIECE // 2
+        starts = [sum(PIECES[:c]) for c in range(len(PIECES))]
         hids = []
-        for c in range(pieces):
+
+        def finish(c):
+            start, width = starts[c], PIECES[c]
+            codes = keep.tile([P, width], U32, name=f"codes{c}", align_bytes=64)
+            scales = keep.tile([P, width], U8, name=f"scales{c}", align_bytes=64)
+            nc.vector.quantize_mx(out=codes[:].bitcast(FP8X4), scales=scales[:], in_=hids[c][:])
+            bank = psum.tile([P, BANK], F32, name="bank")
+            for a in range(N // P):
+                nc.tensor.matmul_mx(
+                    out=bank[:, a * width : (a + 1) * width],
+                    lhsT=w3w[:, 2 * a * P : 2 * (a + 1) * P].bitcast(FP4X4),
+                    lhsT_scale=w3s[:, a * P : (a + 1) * P],
+                    rhs=codes[:].bitcast(FP8X4),
+                    rhs_scale=scales[:],
+                    start=True,
+                    stop=True,
+                )
+            result = keep.tile([P, 2 * width], F32, name=f"result{c}")
+            nc.scalar.copy(out=result[:], in_=bank[:, 0 : 2 * width])
+            nc.sync.dma_start(out=out_view[:, :, start : start + width], in_=result[:].rearrange("p (a n) -> p a n", n=width))
+
+        for c, (start, width) in enumerate(zip(starts, PIECES)):
+            waves = width // 2
             rec = keep.tile([P, waves, PACK], F32, name=f"rec{c}")
             nc.scalar.activation(
-                out=rec[:], in_=lnwave[:, :, c * waves : (c + 1) * waves].rearrange("p t v -> p v t"), func=ACT.Sigmoid, scale=-1.0
+                out=rec[:], in_=lnwave[:, :, start // 2 : start // 2 + waves].rearrange("p t v -> p v t"), func=ACT.Sigmoid, scale=-1.0
             )
-            hid = keep.tile([P, PIECE * PACK], BF16, name=f"hid{c}", align_bytes=64)
+            hid = keep.tile([P, width * PACK], BF16, name=f"hid{c}", align_bytes=64)
             hids.append(hid)
             nc.vector.tensor_tensor(
                 out=hid[:].rearrange("p (v d t) -> p v t d", d=2, t=PACK),
-                in0=prod[:, :, c * PIECE : (c + 1) * PIECE].rearrange("p t (v d) -> p v t d", d=2),
+                in0=prod[:, :, start : start + width].rearrange("p t (v d) -> p v t d", d=2),
                 in1=rec[:].unsqueeze(3).to_broadcast([P, waves, PACK, 2]),
                 op=ALU.mult,
             )
-            for done in ([c - 1] if c > 0 else []) + ([c] if c == pieces - 1 else []):
-                codes = keep.tile([P, PIECE], U32, name=f"codes{done}", align_bytes=64)
-                scales = keep.tile([P, PIECE], U8, name=f"scales{done}", align_bytes=64)
-                nc.vector.quantize_mx(out=codes[:].bitcast(FP8X4), scales=scales[:], in_=hids[done][:])
-                bank = psum.tile([P, BANK], F32, name="bank")
-                for a in range(N // P):
-                    nc.tensor.matmul_mx(
-                        out=bank[:, a * PIECE : (a + 1) * PIECE],
-                        lhsT=w3w[:, 2 * a * P : 2 * (a + 1) * P].bitcast(FP4X4),
-                        lhsT_scale=w3s[:, a * P : (a + 1) * P],
-                        rhs=codes[:].bitcast(FP8X4),
-                        rhs_scale=scales[:],
-                        start=True,
-                        stop=True,
-                    )
-                result = keep.tile([P, BANK], F32, name=f"result{done}")
-                nc.scalar.copy(out=result[:], in_=bank[:])
-                nc.sync.dma_start(
-                    out=out_view[:, :, done * PIECE : (done + 1) * PIECE], in_=result[:].rearrange("p (a n) -> p a n", n=PIECE)
-                )
+            if c > 0:
+                finish(c - 1)
+        finish(len(PIECES) - 1)

@@ -46,7 +46,7 @@ def tile_picked_ygpusch_rel_p_kernel(
         ovl_t = keep.tile([P, S // LIST_ROWS], U16, name="ovl_t")
         xw = keep.tile([P, T], U32, name="xw", align_bytes=64)
         xs = keep.tile([P, T], U8, name="xs", align_bytes=64)
-        raw_w = [keep.tile([P, 2 * H], U8, name=f"raw_w{i}", align_bytes=64) for i in range(2)]
+        raw_w = [keep.tile([P, 2 * H], U8, name="raw_w0", align_bytes=64)]
         raw_s = [keep.tile([P, H], U8, name=f"raw_s{i}", align_bytes=64) for i in range(2)]
 
         for plane in (xs, raw_s[0], raw_s[1]):
@@ -57,35 +57,40 @@ def tile_picked_ygpusch_rel_p_kernel(
         nc.sync.dma_start(out=ovl_t[:], in_=ovl)
         load_scale_rows([nc.sync, nc.sync, nc.scalar, nc.scalar], xs, x_scales)
         nc.sync.dma_start(out=xw[:].bitcast(I32), in_=x_words[0].rearrange("p n t -> p (n t)").bitcast(I32))
-        nc.gpsimd.dma_start(out=raw_w[1][:].bitcast(I32), in_=w2_words[0].bitcast(I32))
         load_scale_rows([nc.sync] * 4, raw_s[0], w1_scales)
         load_scale_rows([nc.sync] * 4, raw_s[1], w2_scales)
 
-        def deal_words(tiles):
-            words = [keep.tile([P, len(tiles), 2 * P], U8, name=f"dealt_w{i}", align_bytes=64) for i in range(2)]
-            for i in range(2):
-                nc.vector.tensor_copy(
-                    out=words[i][:].rearrange("p t (m e) -> p t m e", e=2),
-                    in_=raw_w[i][:].rearrange("p (m t e) -> p t m e", t=PACK, e=2)[:, tiles[0] : tiles[-1] + 1],
-                )
+        def deal_words(i, tiles):
+            words = keep.tile([P, len(tiles), 2 * P], U8, name=f"dealt_w{i}", align_bytes=64)
+            nc.vector.tensor_copy(
+                out=words[:].rearrange("p t (m e) -> p t m e", e=2),
+                in_=raw_w[i][:].rearrange("p (m t e) -> p t m e", t=PACK, e=2)[:, tiles[0] : tiles[-1] + 1],
+            )
             return words
 
-        dealt_w = deal_words(ROUNDS[0])
-        dealt_s = [keep.tile([P, PACK, P], U8, name=f"dealt_s{i}", align_bytes=64) for i in range(2)]
-        for i in range(2):
-            nc.vector.tensor_copy(out=dealt_s[i][:], in_=raw_s[i][:].rearrange("p (m t) -> p t m", t=PACK))
-        w3s = raw_s[1][:, 0:N]
-        load_scale_rows([nc.sync] * 4, w3s, w3_scales)
+        def deal_scales(i):
+            scales = keep.tile([P, PACK, P], U8, name=f"dealt_s{i}", align_bytes=64)
+            nc.vector.tensor_copy(out=scales[:], in_=raw_s[i][:].rearrange("p (m t) -> p t m", t=PACK))
+            return scales
 
         def entries(lst, h):
             cols = BANK // LIST_ROWS
             return lst[:, h * cols : (h + 1) * cols]
 
-        gw = [keep.tile([P, BANK], U32, name=name, align_bytes=64) for name in ("gw0", "raw_s0")]
+        dealt_w = [deal_words(0, ROUNDS[0])]
+        dealt_s = [deal_scales(0)]
         gs = [keep.tile([P, BANK], U8, name=f"gs{h}", align_bytes=64) for h in range(HALVES)]
         for h in range(HALVES):
             nc.vector.tensor_copy(out=gs[h][:], in_=xs[:].indirect(entries(offs_t, h)))
+        gw = [keep.tile([P, BANK], U32, name=name, align_bytes=64) for name in ("gw0", "raw_s0")]
+        for h in range(HALVES):
             nc.vector.tensor_copy(out=gw[h][:], in_=xw[:].indirect(entries(offs_t, h)))
+        raw_w.append(keep.tile([P, 2 * H], U8, name="xs", align_bytes=64))
+        nc.sync.dma_start(out=raw_w[1][:].bitcast(I32), in_=w2_words[0].bitcast(I32))
+        dealt_w.append(deal_words(1, ROUNDS[0]))
+        dealt_s.append(deal_scales(1))
+        w3s = raw_s[1][:, 0:N]
+        load_scale_rows([nc.sync] * 4, w3s, w3_scales)
 
         tflop = keep.tile([P, PACK, S], F32, name="tflop")
         execs = keep.tile([P, PACK, S], F32, name="execs")
@@ -94,7 +99,7 @@ def tile_picked_ygpusch_rel_p_kernel(
 
         spans = [half(0), half(1)]
 
-        unit_t = keep.tile([P, PACK], F32, name="xs", align_bytes=64)
+        unit_t = keep.tile([P, PACK], F32, name="xw", align_bytes=64)
         nc.sync.dma_start(out=unit_t[:], in_=unit.rearrange("(p t) o -> p (t o)", t=PACK))
         prod = keep.tile([P, PACK, S], F32, name="prod")
 
@@ -110,7 +115,7 @@ def tile_picked_ygpusch_rel_p_kernel(
 
         for tiles in ROUNDS:
             if tiles != ROUNDS[0]:
-                dealt_w = deal_words(tiles)
+                dealt_w = [deal_words(i, tiles) for i in range(2)]
                 w3w = raw_w[0][:, 0 : 2 * N]
                 nc.sync.dma_start(out=w3w.bitcast(I32), in_=w3_words[0].bitcast(I32))
             jobs = [(t, i, h) for t in tiles for i in range(2) for h in range(HALVES)]
@@ -178,15 +183,17 @@ def tile_picked_ygpusch_rel_p_kernel(
                     nc.vector.scalar_tensor_tensor(
                         out=rest[:, cols], in0=hidd[:, cols], scalar=-2.0, in1=tflop[:, t, cols], op0=ALU.mult, op1=ALU.add
                     )
-                adder = nc.vector
+                adder = nc.gpsimd if t == tiles[0] else nc.vector
                 for cols in [half(0), half(1)]:
                     adder.tensor_tensor(out=execs[:, t, cols], in0=part[:, cols], in1=rest[:, cols], op=ALU.add)
+                if t == 1:
+                    weigh(0)
         pair_max(PACK - 1)
 
         nc.scalar.activation(out=lnwave[:, 0 : PACK - 1, :], in_=wave[:, 0 : PACK - 1, :], func=ACT.Ln, bias=TINY)
         nc.scalar.activation(out=lnwave[:, PACK - 1, :], in_=wave[:, PACK - 1, :], func=ACT.Ln, bias=TINY)
 
-        for t in range(0, PACK):
+        for t in range(1, PACK):
             weigh(t)
 
         out_view = out.rearrange("(a p) n -> p a n", p=P)

@@ -3,7 +3,7 @@ from contextlib import ExitStack
 import concourse.mybir as mybir
 
 K, T, S, H, N = 512, 2048, 1024, 512, 256
-FLOPS = 2 * K * H * S * 2 + 2 * H * N * S
+FLOPS = 2 * (2 * K * H * S) + 2 * H * N * S
 
 F32 = mybir.dt.float32
 BF16 = mybir.dt.bfloat16
@@ -18,11 +18,17 @@ ACT = mybir.ActivationFunctionType
 
 P = 128
 PACK = 4
+FP4_BYTES = 2
+QUADRANT = 32
+SCALE_ROWS = 4
 BANK = 512
-HALVES = S // BANK
-LIST_ROWS = 16
+PSUM_BANKS = 8
+PER_COLUMN = 16
+PAIR = 2
 TINY = 2.0**-60
+HALVES = [slice(start, start + BANK) for start in range(0, S, BANK)]
 ROUNDS = [(0, 1), (2, 3)]
+VECTOR_SHARE = 512
 PIECES = [256, 256, 256, 128, 128]
 
 
@@ -33,207 +39,238 @@ def tile_picked_ygpusch_rel_p_kernel(
     with ExitStack() as ctx:
         keep = ctx.enter_context(tc.tile_pool(name="keep", bufs=1))
         work = ctx.enter_context(tc.tile_pool(name="work", bufs=2))
-        psum = ctx.enter_context(tc.psum_pool(name="psum", bufs=8))
+        psum = ctx.enter_context(tc.psum_pool(name="psum", bufs=PSUM_BANKS))
 
-        def load_scale_rows(queues, plane, rows):
+        def load_plane(queues, plane, rows):
             for q, queue in enumerate(queues):
-                queue.dma_start(out=plane[32 * q : 32 * q + 4, :].bitcast(I32), in_=rows[0, 4 * q : 4 * q + 4, :].bitcast(I32))
+                queue.dma_start(
+                    out=plane[QUADRANT * q : QUADRANT * q + SCALE_ROWS, :].bitcast(I32),
+                    in_=rows[0, SCALE_ROWS * q : SCALE_ROWS * (q + 1), :].bitcast(I32),
+                )
 
-        def half(h):
-            return slice(h * BANK, (h + 1) * BANK)
+        def entries(list_tile, start, stop):
+            return list_tile[:, start // PER_COLUMN : stop // PER_COLUMN]
 
-        offs_t = keep.tile([P, S // LIST_ROWS], U16, name="offs_t")
-        ovl_t = keep.tile([P, S // LIST_ROWS], U16, name="ovl_t")
-        xw = keep.tile([P, T], U32, name="xw", align_bytes=64)
-        xs = keep.tile([P, T], U8, name="xs", align_bytes=64)
-        raw_w = [keep.tile([P, 2 * H], U8, name="raw_w0", align_bytes=64)]
-        raw_s = [keep.tile([P, H], U8, name=f"raw_s{i}", align_bytes=64) for i in range(2)]
+        offs_tile = keep.tile([P, S // PER_COLUMN], U16, name="offs_tile")
+        ovl_tile = keep.tile([P, S // PER_COLUMN], U16, name="ovl_tile")
+        x_word_table = keep.tile([P, T], U32, name="x_word_table", tag="x_word_bytes", align_bytes=64)
+        x_scale_table = keep.tile([P, T], U8, name="x_scale_table", tag="x_scale_bytes", align_bytes=64)
+        w1_loaded = keep.tile([P, FP4_BYTES * H], U8, name="w1_loaded", align_bytes=64)
+        w1_plane = keep.tile([P, H], U8, name="w1_plane", tag="w1_plane_bytes", align_bytes=64)
+        w2_plane = keep.tile([P, H], U8, name="w2_plane", align_bytes=64)
 
-        for plane in (xs, raw_s[0], raw_s[1]):
-            nc.vector.memset(plane[:].bitcast(I32), 0)
+        nc.gpsimd.memset(x_scale_table[:, 0 : T // 2].bitcast(I32), 0)
+        for plane in (x_scale_table[:, T // 2 : T], w1_plane[:], w2_plane[:]):
+            nc.vector.memset(plane.bitcast(I32), 0)
 
-        nc.sync.dma_start(out=raw_w[0][:].bitcast(I32), in_=w1_words[0].bitcast(I32))
-        nc.sync.dma_start(out=offs_t[:], in_=offs)
-        nc.sync.dma_start(out=ovl_t[:], in_=ovl)
-        load_scale_rows([nc.sync, nc.sync, nc.scalar, nc.scalar], xs, x_scales)
-        nc.sync.dma_start(out=xw[:].bitcast(I32), in_=x_words[0].rearrange("p n t -> p (n t)").bitcast(I32))
-        load_scale_rows([nc.sync] * 4, raw_s[0], w1_scales)
-        load_scale_rows([nc.sync] * 4, raw_s[1], w2_scales)
+        nc.sync.dma_start(out=w1_loaded[:].bitcast(I32), in_=w1_words[0].bitcast(I32))
+        nc.sync.dma_start(out=offs_tile[:], in_=offs)
+        nc.sync.dma_start(out=ovl_tile[:], in_=ovl)
+        load_plane([nc.sync, nc.sync, nc.scalar, nc.scalar], x_scale_table, x_scales)
+        nc.sync.dma_start(out=x_word_table[:].bitcast(I32), in_=x_words[0].rearrange("p n t -> p (n t)").bitcast(I32))
+        load_plane([nc.sync] * 4, w1_plane, w1_scales)
+        load_plane([nc.sync] * 4, w2_plane, w2_scales)
 
-        def deal_words(i, tiles):
-            words = keep.tile([P, len(tiles), 2 * P], U8, name=f"dealt_w{i}", align_bytes=64)
+        def deal_words(loaded, slots, name):
+            dealt = keep.tile([P, len(slots), FP4_BYTES * P], U8, name=name, align_bytes=64)
             nc.vector.tensor_copy(
-                out=words[:].rearrange("p t (m e) -> p t m e", e=2),
-                in_=raw_w[i][:].rearrange("p (m t e) -> p t m e", t=PACK, e=2)[:, tiles[0] : tiles[-1] + 1],
+                out=dealt[:].rearrange("p t (m e) -> p t m e", e=FP4_BYTES),
+                in_=loaded[:].rearrange("p (m t e) -> p t m e", t=PACK, e=FP4_BYTES)[:, slots[0] : slots[-1] + 1],
             )
-            return words
+            return dealt
 
-        def deal_scales(i):
-            scales = keep.tile([P, PACK, P], U8, name=f"dealt_s{i}", align_bytes=64)
-            nc.vector.tensor_copy(out=scales[:], in_=raw_s[i][:].rearrange("p (m t) -> p t m", t=PACK))
-            return scales
+        def deal_scales(plane, name):
+            dealt = keep.tile([P, PACK, P], U8, name=name, align_bytes=64)
+            nc.vector.tensor_copy(out=dealt[:], in_=plane[:].rearrange("p (m t) -> p t m", t=PACK))
+            return dealt
 
-        def entries(lst, h):
-            cols = BANK // LIST_ROWS
-            return lst[:, h * cols : (h + 1) * cols]
+        w1_dealt = deal_words(w1_loaded, ROUNDS[0], "w1_dealt")
+        w1_dealt_scales = deal_scales(w1_plane, "w1_dealt_scales")
 
-        dealt_w = [deal_words(0, ROUNDS[0])]
-        dealt_s = [deal_scales(0)]
-        gs = [keep.tile([P, BANK], U8, name=f"gs{h}", align_bytes=64) for h in range(HALVES)]
-        for h in range(HALVES):
-            nc.vector.tensor_copy(out=gs[h][:], in_=xs[:].indirect(entries(offs_t, h)))
-        gw = [keep.tile([P, BANK], U32, name=name, align_bytes=64) for name in ("gw0", "raw_s0")]
-        for h in range(HALVES):
-            nc.vector.tensor_copy(out=gw[h][:], in_=xw[:].indirect(entries(offs_t, h)))
-        raw_w.append(keep.tile([P, 2 * H], U8, name="xs", align_bytes=64))
-        nc.sync.dma_start(out=raw_w[1][:].bitcast(I32), in_=w2_words[0].bitcast(I32))
-        dealt_w.append(deal_words(1, ROUNDS[0]))
-        dealt_s.append(deal_scales(1))
-        w3s = raw_s[1][:, 0:N]
-        load_scale_rows([nc.sync] * 4, w3s, w3_scales)
+        picked_scales = [keep.tile([P, BANK], U8, name=f"picked_scales{h}", align_bytes=64) for h in range(len(HALVES))]
+        for cols, picked in zip(HALVES, picked_scales):
+            nc.vector.tensor_copy(out=picked[:], in_=x_scale_table[:].indirect(entries(offs_tile, cols.start, cols.stop)))
+        picked_words = [
+            keep.tile([P, BANK], U32, name="picked_words0", align_bytes=64),
+            keep.tile([P, BANK], U32, name="picked_words1", tag="w1_plane_bytes", align_bytes=64),
+        ]
+        for cols, picked in zip(HALVES, picked_words):
+            nc.vector.tensor_copy(out=picked[:], in_=x_word_table[:].indirect(entries(offs_tile, cols.start, cols.stop)))
+
+        w2_loaded = keep.tile([P, FP4_BYTES * H], U8, name="w2_loaded", tag="x_scale_bytes", align_bytes=64)
+        nc.sync.dma_start(out=w2_loaded[:].bitcast(I32), in_=w2_words[0].bitcast(I32))
+        w2_dealt = deal_words(w2_loaded, ROUNDS[0], "w2_dealt")
+        w2_dealt_scales = deal_scales(w2_plane, "w2_dealt_scales")
+        w3_plane = w2_plane[:, 0:N]
+        load_plane([nc.sync] * 4, w3_plane, w3_scales)
 
         tflop = keep.tile([P, PACK, S], F32, name="tflop")
-        execs = keep.tile([P, PACK, S], F32, name="execs")
-        wave = keep.tile([P, PACK, S // 2], F32, name="wave")
-        lnwave = keep.tile([P, PACK, S // 2], F32, name="lnwave")
-
-        spans = [half(0), half(1)]
-
-        unit_t = keep.tile([P, PACK], F32, name="xw", align_bytes=64)
-        nc.sync.dma_start(out=unit_t[:], in_=unit.rearrange("(p t) o -> p (t o)", t=PACK))
-        prod = keep.tile([P, PACK, S], F32, name="prod")
+        busy = keep.tile([P, PACK, S], F32, name="busy")
+        peak = keep.tile([P, PACK, S // PAIR], F32, name="peak")
+        ln_peak = keep.tile([P, PACK, S // PAIR], F32, name="ln_peak")
+        unit_tile = keep.tile([P, PACK], F32, name="unit_tile", tag="x_word_bytes", align_bytes=64)
+        nc.sync.dma_start(out=unit_tile[:], in_=unit.rearrange("(p t) o -> p (t o)", t=PACK))
+        weighted = keep.tile([P, PACK, S], F32, name="weighted")
 
         def weigh(t):
             nc.vector.scalar_tensor_tensor(
-                out=prod[:, t, :], in0=execs[:, t, :], scalar=unit_t[:, t : t + 1], in1=tflop[:, t, :], op0=ALU.mult, op1=ALU.mult
+                out=weighted[:, t, :], in0=busy[:, t, :], scalar=unit_tile[:, t : t + 1], in1=tflop[:, t, :], op0=ALU.mult, op1=ALU.mult
             )
 
         def pair_max(t):
-            for cols in spans:
-                pairs = execs[:, t, cols].rearrange("p (v d) -> p v d", d=2)
-                nc.vector.tensor_tensor(out=wave[:, t, cols.start // 2 : cols.stop // 2], in0=pairs[:, :, 0], in1=pairs[:, :, 1], op=ALU.max)
+            for cols in HALVES:
+                pairs = busy[:, t, cols].rearrange("p (v d) -> p v d", d=PAIR)
+                nc.vector.tensor_tensor(
+                    out=peak[:, t, cols.start // PAIR : cols.stop // PAIR], in0=pairs[:, :, 0], in1=pairs[:, :, 1], op=ALU.max
+                )
 
-        for tiles in ROUNDS:
-            if tiles != ROUNDS[0]:
-                dealt_w = [deal_words(i, tiles) for i in range(2)]
-                w3w = raw_w[0][:, 0 : 2 * N]
-                nc.sync.dma_start(out=w3w.bitcast(I32), in_=w3_words[0].bitcast(I32))
-            jobs = [(t, i, h) for t in tiles for i in range(2) for h in range(HALVES)]
-            nb = len(jobs)
-            share = BANK // nb
-            row = share + BANK
-            sig = work.tile([P, nb * row], F32, name="sig")
-            lns = sig
+        share = BANK // PSUM_BANKS
+        row = share + BANK
+        last = PSUM_BANKS - 1
 
-            def place(tile, k):
-                if k < nb - 1:
-                    return tile[:, k * row + share : (k + 1) * row]
-                return tile[:].rearrange("p (k r) -> p k r", r=row)[:, :, 0:share]
+        def staged(stage, k):
+            if k < last:
+                return stage[:, k * row + share : (k + 1) * row]
+            return stage[:].rearrange("p (k r) -> p k r", r=row)[:, :, 0:share]
 
-            def shaped(ap, k):
-                return ap if k < nb - 1 else ap.rearrange("p (k r) -> p k r", r=share)
+        def like_staged(columns, k):
+            return columns if k < last else columns.rearrange("p (k r) -> p k r", r=share)
 
+        for slots in ROUNDS:
+            first_round = slots == ROUNDS[0]
+            if not first_round:
+                w1_dealt = deal_words(w1_loaded, slots, "w1_dealt")
+                w2_dealt = deal_words(w2_loaded, slots, "w2_dealt")
+                w3_loaded = w1_loaded[:, 0 : FP4_BYTES * N]
+                nc.sync.dma_start(out=w3_loaded.bitcast(I32), in_=w3_words[0].bitcast(I32))
+            weights = [(w1_dealt, w1_dealt_scales), (w2_dealt, w2_dealt_scales)]
+            jobs = [(t, i, h) for t in slots for i in range(2) for h in range(len(HALVES))]
+            stage = work.tile([P, PSUM_BANKS * row], F32, name="stage")
+
+            order = list(range(PSUM_BANKS))
+            if first_round:
+                order = sorted(order, key=lambda k: (jobs[k][2], jobs[k][1]))
             banks = {}
-            for k in sorted(range(nb), key=lambda k: (jobs[k][2], jobs[k][1]) if tiles == ROUNDS[0] else k):
+            for k in order:
                 t, i, h = jobs[k]
-                bank = psum.tile([P, BANK], F32, name="bank")
-                banks[k] = bank
+                dealt, dealt_scales = weights[i]
+                banks[k] = psum.tile([P, BANK], F32, name="bank")
                 nc.tensor.matmul_mx(
-                    out=bank[:],
-                    lhsT=dealt_w[i][:, t - tiles[0], :].bitcast(FP4X4),
-                    lhsT_scale=dealt_s[i][:, t, :],
-                    rhs=gw[h][:].bitcast(FP8X4),
-                    rhs_scale=gs[h][:],
+                    out=banks[k][:],
+                    lhsT=dealt[:, t - slots[0], :].bitcast(FP4X4),
+                    lhsT_scale=dealt_scales[:, t, :],
+                    rhs=picked_words[h][:].bitcast(FP8X4),
+                    rhs_scale=picked_scales[h][:],
                     start=True,
                     stop=True,
                 )
-                nc.scalar.activation(out=place(sig, k), in_=shaped(bank[:], k), func=ACT.Sigmoid, scale=-1.0)
+                nc.scalar.activation(out=staged(stage, k), in_=like_staged(banks[k][:], k), func=ACT.Sigmoid, scale=-1.0)
 
-            for t in tiles:
+            for t in slots:
                 tmem = work.tile([P, S], F32, name="tmem")
                 tmo = work.tile([P, S], F32, name="tmo")
                 roof = work.tile([P, S], F32, name="roof")
-                part = work.tile([P, S], F32, name="part")
+                own_part = work.tile([P, S], F32, name="own_part")
                 hidd = work.tile([P, S], F32, name="hidd")
-                rest = work.tile([P, S], F32, name="rest")
-                mine = [k for k, job in enumerate(jobs) if job[0] == t]
-                for k in mine:
-                    if k < nb - 1:
-                        cols = slice(k * row, (k + 1) * row + (share if k == nb - 2 else 0))
-                        nc.scalar.activation(out=lns[:, cols], in_=sig[:, cols], func=ACT.Ln, bias=TINY)
-                for k in mine:
+                overlap_part = work.tile([P, S], F32, name="overlap_part")
+                own_banks = [k for k, job in enumerate(jobs) if job[0] == t]
+
+                for k in own_banks:
+                    if k < last:
+                        run = slice(k * row, (k + 1) * row + (share if k == last - 1 else 0))
+                        nc.scalar.activation(out=stage[:, run], in_=stage[:, run], func=ACT.Ln, bias=TINY)
+                for k in own_banks:
                     i, h = jobs[k][1:]
-                    target = tmem[:, half(h)] if i == 0 else tflop[:, t, half(h)]
+                    target = tmem[:, HALVES[h]] if i == 0 else tflop[:, t, HALVES[h]]
                     nc.vector.scalar_tensor_tensor(
-                        out=shaped(target, k), in0=place(lns, k), scalar=-1.0, in1=shaped(banks[k][:], k), op0=ALU.mult, op1=ALU.max
+                        out=like_staged(target, k),
+                        in0=staged(stage, k),
+                        scalar=-1.0,
+                        in1=like_staged(banks[k][:], k),
+                        op0=ALU.mult,
+                        op1=ALU.max,
                     )
-                for h in range(HALVES):
-                    nc.scalar.activation(out=tmo[:, half(h)], in_=tmem[:].indirect(entries(ovl_t, h)), func=ACT.Copy)
+
+                ends_first_round = t == ROUNDS[0][-1]
+                on_scalar = S - VECTOR_SHARE if ends_first_round else S
+                for start in range(0, on_scalar, BANK):
+                    nc.scalar.activation(
+                        out=tmo[:, start : start + BANK], in_=tmem[:].indirect(entries(ovl_tile, start, start + BANK)), func=ACT.Copy
+                    )
+                if ends_first_round:
+                    nc.vector.tensor_copy(out=tmo[:, on_scalar:S], in_=tmem[:].indirect(entries(ovl_tile, on_scalar, S)))
+
                 if t > 0:
                     pair_max(t - 1)
-                for cols in spans:
+                for cols in HALVES:
                     nc.vector.tensor_tensor(out=roof[:, cols], in0=tmem[:, cols], in1=tflop[:, t, cols], op=ALU.max)
-                for cols in spans:
+                for cols in HALVES:
                     nc.vector.scalar_tensor_tensor(
-                        out=part[:, cols], in0=roof[:, cols], scalar=0.7 / 0.3, in1=tmem[:, cols], op0=ALU.mult, op1=ALU.add
+                        out=own_part[:, cols], in0=roof[:, cols], scalar=0.7 / 0.3, in1=tmem[:, cols], op0=ALU.mult, op1=ALU.add
                     )
-                for cols in spans:
-                    nc.vector.tensor_tensor(out=hidd[:, cols], in0=tmo[:, cols], in1=tflop[:, t, cols], op=ALU.min)
-                for cols in spans:
-                    nc.vector.scalar_tensor_tensor(
-                        out=rest[:, cols], in0=hidd[:, cols], scalar=-2.0, in1=tflop[:, t, cols], op0=ALU.mult, op1=ALU.add
-                    )
-                adder = nc.gpsimd if t == tiles[0] else nc.vector
-                for cols in [half(0), half(1)]:
-                    adder.tensor_tensor(out=execs[:, t, cols], in0=part[:, cols], in1=rest[:, cols], op=ALU.add)
-                if t == 1:
+                if ends_first_round:
                     weigh(0)
+                for cols in HALVES:
+                    nc.vector.tensor_tensor(out=hidd[:, cols], in0=tmo[:, cols], in1=tflop[:, t, cols], op=ALU.min)
+                for cols in HALVES:
+                    nc.vector.scalar_tensor_tensor(
+                        out=overlap_part[:, cols], in0=hidd[:, cols], scalar=-0.6 / 0.3, in1=tflop[:, t, cols], op0=ALU.mult, op1=ALU.add
+                    )
+                adder = nc.gpsimd if t < PACK - 1 else nc.vector
+                for cols in HALVES:
+                    adder.tensor_tensor(out=busy[:, t, cols], in0=own_part[:, cols], in1=overlap_part[:, cols], op=ALU.add)
         pair_max(PACK - 1)
 
-        nc.scalar.activation(out=lnwave[:, 0 : PACK - 1, :], in_=wave[:, 0 : PACK - 1, :], func=ACT.Ln, bias=TINY)
-        nc.scalar.activation(out=lnwave[:, PACK - 1, :], in_=wave[:, PACK - 1, :], func=ACT.Ln, bias=TINY)
-
+        nc.scalar.activation(out=ln_peak[:, 0 : PACK - 1, :], in_=peak[:, 0 : PACK - 1, :], func=ACT.Ln, bias=TINY)
+        nc.scalar.activation(out=ln_peak[:, PACK - 1, :], in_=peak[:, PACK - 1, :], func=ACT.Ln, bias=TINY)
         for t in range(1, PACK):
             weigh(t)
 
-        out_view = out.rearrange("(a p) n -> p a n", p=P)
-        starts = [sum(PIECES[:c]) for c in range(len(PIECES))]
-        hids = []
+        out_rows = out.rearrange("(a p) n -> p a n", p=P)
+        row_tiles = N // P
 
-        def finish(c):
-            start, width = starts[c], PIECES[c]
+        def make_hid(c, start, width):
+            waves = width // PAIR
+            inverse = keep.tile([P, waves, PACK], F32, name=f"inverse{c}")
+            nc.scalar.activation(
+                out=inverse[:],
+                in_=ln_peak[:, :, start // PAIR : start // PAIR + waves].rearrange("p t v -> p v t"),
+                func=ACT.Sigmoid,
+                scale=-1.0,
+            )
+            hid = keep.tile([P, width * PACK], BF16, name=f"hid{c}", align_bytes=64)
+            nc.vector.tensor_tensor(
+                out=hid[:].rearrange("p (v d t) -> p v t d", d=PAIR, t=PACK),
+                in0=weighted[:, :, start : start + width].rearrange("p t (v d) -> p v t d", d=PAIR),
+                in1=inverse[:].unsqueeze(3).to_broadcast([P, waves, PACK, PAIR]),
+                op=ALU.mult,
+            )
+            return hid
+
+        def finish(c, start, width, hid):
             codes = keep.tile([P, width], U32, name=f"codes{c}", align_bytes=64)
-            scales = keep.tile([P, width], U8, name=f"scales{c}", align_bytes=64)
-            nc.vector.quantize_mx(out=codes[:].bitcast(FP8X4), scales=scales[:], in_=hids[c][:])
+            hid_plane = keep.tile([P, width], U8, name=f"hid_plane{c}", align_bytes=64)
+            nc.vector.quantize_mx(out=codes[:].bitcast(FP8X4), scales=hid_plane[:], in_=hid[:])
             bank = psum.tile([P, BANK], F32, name="bank")
-            for a in range(N // P):
+            for a in range(row_tiles):
                 nc.tensor.matmul_mx(
                     out=bank[:, a * width : (a + 1) * width],
-                    lhsT=w3w[:, 2 * a * P : 2 * (a + 1) * P].bitcast(FP4X4),
-                    lhsT_scale=w3s[:, a * P : (a + 1) * P],
+                    lhsT=w3_loaded[:, FP4_BYTES * a * P : FP4_BYTES * (a + 1) * P].bitcast(FP4X4),
+                    lhsT_scale=w3_plane[:, a * P : (a + 1) * P],
                     rhs=codes[:].bitcast(FP8X4),
-                    rhs_scale=scales[:],
+                    rhs_scale=hid_plane[:],
                     start=True,
                     stop=True,
                 )
-            result = keep.tile([P, 2 * width], F32, name=f"result{c}")
-            nc.scalar.copy(out=result[:], in_=bank[:, 0 : 2 * width])
-            nc.sync.dma_start(out=out_view[:, :, start : start + width], in_=result[:].rearrange("p (a n) -> p a n", n=width))
+            result = keep.tile([P, row_tiles * width], F32, name=f"result{c}")
+            nc.scalar.copy(out=result[:], in_=bank[:, 0 : row_tiles * width])
+            nc.sync.dma_start(out=out_rows[:, :, start : start + width], in_=result[:].rearrange("p (a n) -> p a n", n=width))
 
-        for c, (start, width) in enumerate(zip(starts, PIECES)):
-            waves = width // 2
-            rec = keep.tile([P, waves, PACK], F32, name=f"rec{c}")
-            nc.scalar.activation(
-                out=rec[:], in_=lnwave[:, :, start // 2 : start // 2 + waves].rearrange("p t v -> p v t"), func=ACT.Sigmoid, scale=-1.0
-            )
-            hid = keep.tile([P, width * PACK], BF16, name=f"hid{c}", align_bytes=64)
-            hids.append(hid)
-            nc.vector.tensor_tensor(
-                out=hid[:].rearrange("p (v d t) -> p v t d", d=2, t=PACK),
-                in0=prod[:, :, start : start + width].rearrange("p t (v d) -> p v t d", d=2),
-                in1=rec[:].unsqueeze(3).to_broadcast([P, waves, PACK, 2]),
-                op=ALU.mult,
-            )
-            if c > 0:
-                finish(c - 1)
-        finish(len(PIECES) - 1)
+        waiting = None
+        for c, width in enumerate(PIECES):
+            start = sum(PIECES[:c])
+            hid = make_hid(c, start, width)
+            if waiting is not None:
+                finish(*waiting)
+            waiting = (c, start, width, hid)
+        finish(*waiting)

from contextlib import ExitStack

import concourse.mybir as mybir

K, T, S, H, N = 512, 2048, 1024, 512, 256
FLOPS = 2 * (2 * K * H * S) + 2 * H * N * S

F32 = mybir.dt.float32
BF16 = mybir.dt.bfloat16
I32 = mybir.dt.int32
U32 = mybir.dt.uint32
U16 = mybir.dt.uint16
U8 = mybir.dt.uint8
FP8X4 = mybir.dt.float8_e4m3fn_x4
FP4X4 = mybir.dt.float4_e2m1fn_x4
ALU = mybir.AluOpType
ACT = mybir.ActivationFunctionType

P = 128
PACK = 4
FP4_BYTES = 2
QUADRANT = 32
SCALE_ROWS = 4
BANK = 512
PSUM_BANKS = 8
PER_COLUMN = 16
PAIR = 2
TINY = 2.0**-60
HALVES = [slice(start, start + BANK) for start in range(0, S, BANK)]
ROUNDS = [(0, 1), (2, 3)]
VECTOR_SHARE = 512
PIECES = [256, 256, 256, 128, 128]


def tile_picked_ygpusch_rel_p_kernel(
    tc, x_words, x_scales, w1_words, w1_scales, w2_words, w2_scales, unit, w3_words, w3_scales, offs, ovl, out
):
    nc = tc.nc
    with ExitStack() as ctx:
        keep = ctx.enter_context(tc.tile_pool(name="keep", bufs=1))
        work = ctx.enter_context(tc.tile_pool(name="work", bufs=2))
        psum = ctx.enter_context(tc.psum_pool(name="psum", bufs=PSUM_BANKS))

        def load_plane(queues, plane, rows):
            for q, queue in enumerate(queues):
                queue.dma_start(
                    out=plane[QUADRANT * q : QUADRANT * q + SCALE_ROWS, :].bitcast(I32),
                    in_=rows[0, SCALE_ROWS * q : SCALE_ROWS * (q + 1), :].bitcast(I32),
                )

        def entries(list_tile, start, stop):
            return list_tile[:, start // PER_COLUMN : stop // PER_COLUMN]

        offs_tile = keep.tile([P, S // PER_COLUMN], U16, name="offs_tile")
        ovl_tile = keep.tile([P, S // PER_COLUMN], U16, name="ovl_tile")
        x_word_table = keep.tile([P, T], U32, name="x_word_table", tag="x_word_bytes", align_bytes=64)
        x_scale_table = keep.tile([P, T], U8, name="x_scale_table", tag="x_scale_bytes", align_bytes=64)
        w1_loaded = keep.tile([P, FP4_BYTES * H], U8, name="w1_loaded", align_bytes=64)
        w1_plane = keep.tile([P, H], U8, name="w1_plane", tag="w1_plane_bytes", align_bytes=64)
        w2_plane = keep.tile([P, H], U8, name="w2_plane", align_bytes=64)

        nc.gpsimd.memset(x_scale_table[:, 0 : T // 2].bitcast(I32), 0)
        for plane in (x_scale_table[:, T // 2 : T], w1_plane[:], w2_plane[:]):
            nc.vector.memset(plane.bitcast(I32), 0)

        nc.sync.dma_start(out=w1_loaded[:].bitcast(I32), in_=w1_words[0].bitcast(I32))
        nc.sync.dma_start(out=offs_tile[:], in_=offs)
        nc.sync.dma_start(out=ovl_tile[:], in_=ovl)
        load_plane([nc.sync, nc.sync, nc.scalar, nc.scalar], x_scale_table, x_scales)
        nc.sync.dma_start(out=x_word_table[:].bitcast(I32), in_=x_words[0].rearrange("p n t -> p (n t)").bitcast(I32))
        load_plane([nc.sync] * 4, w1_plane, w1_scales)
        load_plane([nc.sync] * 4, w2_plane, w2_scales)

        def deal_words(loaded, slots, name):
            dealt = keep.tile([P, len(slots), FP4_BYTES * P], U8, name=name, align_bytes=64)
            nc.vector.tensor_copy(
                out=dealt[:].rearrange("p t (m e) -> p t m e", e=FP4_BYTES),
                in_=loaded[:].rearrange("p (m t e) -> p t m e", t=PACK, e=FP4_BYTES)[:, slots[0] : slots[-1] + 1],
            )
            return dealt

        def deal_scales(plane, name):
            dealt = keep.tile([P, PACK, P], U8, name=name, align_bytes=64)
            nc.vector.tensor_copy(out=dealt[:], in_=plane[:].rearrange("p (m t) -> p t m", t=PACK))
            return dealt

        w1_dealt = deal_words(w1_loaded, ROUNDS[0], "w1_dealt")
        w1_dealt_scales = deal_scales(w1_plane, "w1_dealt_scales")

        picked_scales = [keep.tile([P, BANK], U8, name=f"picked_scales{h}", align_bytes=64) for h in range(len(HALVES))]
        for cols, picked in zip(HALVES, picked_scales):
            nc.vector.tensor_copy(out=picked[:], in_=x_scale_table[:].indirect(entries(offs_tile, cols.start, cols.stop)))
        picked_words = [
            keep.tile([P, BANK], U32, name="picked_words0", align_bytes=64),
            keep.tile([P, BANK], U32, name="picked_words1", tag="w1_plane_bytes", align_bytes=64),
        ]
        for cols, picked in zip(HALVES, picked_words):
            nc.vector.tensor_copy(out=picked[:], in_=x_word_table[:].indirect(entries(offs_tile, cols.start, cols.stop)))

        w2_loaded = keep.tile([P, FP4_BYTES * H], U8, name="w2_loaded", tag="x_scale_bytes", align_bytes=64)
        nc.sync.dma_start(out=w2_loaded[:].bitcast(I32), in_=w2_words[0].bitcast(I32))
        w2_dealt = deal_words(w2_loaded, ROUNDS[0], "w2_dealt")
        w2_dealt_scales = deal_scales(w2_plane, "w2_dealt_scales")
        w3_plane = w2_plane[:, 0:N]
        load_plane([nc.sync] * 4, w3_plane, w3_scales)

        tflop = keep.tile([P, PACK, S], F32, name="tflop")
        busy = keep.tile([P, PACK, S], F32, name="busy")
        peak = keep.tile([P, PACK, S // PAIR], F32, name="peak")
        ln_peak = keep.tile([P, PACK, S // PAIR], F32, name="ln_peak")
        unit_tile = keep.tile([P, PACK], F32, name="unit_tile", tag="x_word_bytes", align_bytes=64)
        nc.sync.dma_start(out=unit_tile[:], in_=unit.rearrange("(p t) o -> p (t o)", t=PACK))
        weighted = keep.tile([P, PACK, S], F32, name="weighted")

        def weigh(t):
            nc.vector.scalar_tensor_tensor(
                out=weighted[:, t, :], in0=busy[:, t, :], scalar=unit_tile[:, t : t + 1], in1=tflop[:, t, :], op0=ALU.mult, op1=ALU.mult
            )

        def pair_max(t):
            for cols in HALVES:
                pairs = busy[:, t, cols].rearrange("p (v d) -> p v d", d=PAIR)
                nc.vector.tensor_tensor(
                    out=peak[:, t, cols.start // PAIR : cols.stop // PAIR], in0=pairs[:, :, 0], in1=pairs[:, :, 1], op=ALU.max
                )

        share = BANK // PSUM_BANKS
        row = share + BANK
        last = PSUM_BANKS - 1

        def staged(stage, k):
            if k < last:
                return stage[:, k * row + share : (k + 1) * row]
            return stage[:].rearrange("p (k r) -> p k r", r=row)[:, :, 0:share]

        def like_staged(columns, k):
            return columns if k < last else columns.rearrange("p (k r) -> p k r", r=share)

        for slots in ROUNDS:
            first_round = slots == ROUNDS[0]
            if not first_round:
                w1_dealt = deal_words(w1_loaded, slots, "w1_dealt")
                w2_dealt = deal_words(w2_loaded, slots, "w2_dealt")
                w3_loaded = w1_loaded[:, 0 : FP4_BYTES * N]
                nc.sync.dma_start(out=w3_loaded.bitcast(I32), in_=w3_words[0].bitcast(I32))
            weights = [(w1_dealt, w1_dealt_scales), (w2_dealt, w2_dealt_scales)]
            jobs = [(t, i, h) for t in slots for i in range(2) for h in range(len(HALVES))]
            stage = work.tile([P, PSUM_BANKS * row], F32, name="stage")

            order = list(range(PSUM_BANKS))
            if first_round:
                order = sorted(order, key=lambda k: (jobs[k][2], jobs[k][1]))
            banks = {}
            for k in order:
                t, i, h = jobs[k]
                dealt, dealt_scales = weights[i]
                banks[k] = psum.tile([P, BANK], F32, name="bank")
                nc.tensor.matmul_mx(
                    out=banks[k][:],
                    lhsT=dealt[:, t - slots[0], :].bitcast(FP4X4),
                    lhsT_scale=dealt_scales[:, t, :],
                    rhs=picked_words[h][:].bitcast(FP8X4),
                    rhs_scale=picked_scales[h][:],
                    start=True,
                    stop=True,
                )
                nc.scalar.activation(out=staged(stage, k), in_=like_staged(banks[k][:], k), func=ACT.Sigmoid, scale=-1.0)

            for t in slots:
                tmem = work.tile([P, S], F32, name="tmem")
                tmo = work.tile([P, S], F32, name="tmo")
                roof = work.tile([P, S], F32, name="roof")
                own_part = work.tile([P, S], F32, name="own_part")
                hidd = work.tile([P, S], F32, name="hidd")
                overlap_part = work.tile([P, S], F32, name="overlap_part")
                own_banks = [k for k, job in enumerate(jobs) if job[0] == t]

                for k in own_banks:
                    if k < last:
                        run = slice(k * row, (k + 1) * row + (share if k == last - 1 else 0))
                        nc.scalar.activation(out=stage[:, run], in_=stage[:, run], func=ACT.Ln, bias=TINY)
                for k in own_banks:
                    i, h = jobs[k][1:]
                    target = tmem[:, HALVES[h]] if i == 0 else tflop[:, t, HALVES[h]]
                    nc.vector.scalar_tensor_tensor(
                        out=like_staged(target, k),
                        in0=staged(stage, k),
                        scalar=-1.0,
                        in1=like_staged(banks[k][:], k),
                        op0=ALU.mult,
                        op1=ALU.max,
                    )

                ends_first_round = t == ROUNDS[0][-1]
                on_scalar = S - VECTOR_SHARE if ends_first_round else S
                for start in range(0, on_scalar, BANK):
                    nc.scalar.activation(
                        out=tmo[:, start : start + BANK], in_=tmem[:].indirect(entries(ovl_tile, start, start + BANK)), func=ACT.Copy
                    )
                if ends_first_round:
                    nc.vector.tensor_copy(out=tmo[:, on_scalar:S], in_=tmem[:].indirect(entries(ovl_tile, on_scalar, S)))

                if t > 0:
                    pair_max(t - 1)
                for cols in HALVES:
                    nc.vector.tensor_tensor(out=roof[:, cols], in0=tmem[:, cols], in1=tflop[:, t, cols], op=ALU.max)
                for cols in HALVES:
                    nc.vector.scalar_tensor_tensor(
                        out=own_part[:, cols], in0=roof[:, cols], scalar=0.7 / 0.3, in1=tmem[:, cols], op0=ALU.mult, op1=ALU.add
                    )
                if ends_first_round:
                    weigh(0)
                for cols in HALVES:
                    nc.vector.tensor_tensor(out=hidd[:, cols], in0=tmo[:, cols], in1=tflop[:, t, cols], op=ALU.min)
                for cols in HALVES:
                    nc.vector.scalar_tensor_tensor(
                        out=overlap_part[:, cols], in0=hidd[:, cols], scalar=-0.6 / 0.3, in1=tflop[:, t, cols], op0=ALU.mult, op1=ALU.add
                    )
                adder = nc.gpsimd if t < PACK - 1 else nc.vector
                for cols in HALVES:
                    adder.tensor_tensor(out=busy[:, t, cols], in0=own_part[:, cols], in1=overlap_part[:, cols], op=ALU.add)
        pair_max(PACK - 1)

        nc.scalar.activation(out=ln_peak[:, 0 : PACK - 1, :], in_=peak[:, 0 : PACK - 1, :], func=ACT.Ln, bias=TINY)
        nc.scalar.activation(out=ln_peak[:, PACK - 1, :], in_=peak[:, PACK - 1, :], func=ACT.Ln, bias=TINY)
        for t in range(1, PACK):
            weigh(t)

        out_rows = out.rearrange("(a p) n -> p a n", p=P)
        row_tiles = N // P

        def make_hid(c, start, width):
            waves = width // PAIR
            inverse = keep.tile([P, waves, PACK], F32, name=f"inverse{c}")
            nc.scalar.activation(
                out=inverse[:],
                in_=ln_peak[:, :, start // PAIR : start // PAIR + waves].rearrange("p t v -> p v t"),
                func=ACT.Sigmoid,
                scale=-1.0,
            )
            hid = keep.tile([P, width * PACK], BF16, name=f"hid{c}", align_bytes=64)
            nc.vector.tensor_tensor(
                out=hid[:].rearrange("p (v d t) -> p v t d", d=PAIR, t=PACK),
                in0=weighted[:, :, start : start + width].rearrange("p t (v d) -> p v t d", d=PAIR),
                in1=inverse[:].unsqueeze(3).to_broadcast([P, waves, PACK, PAIR]),
                op=ALU.mult,
            )
            return hid

        def finish(c, start, width, hid):
            codes = keep.tile([P, width], U32, name=f"codes{c}", align_bytes=64)
            hid_plane = keep.tile([P, width], U8, name=f"hid_plane{c}", align_bytes=64)
            nc.vector.quantize_mx(out=codes[:].bitcast(FP8X4), scales=hid_plane[:], in_=hid[:])
            bank = psum.tile([P, BANK], F32, name="bank")
            for a in range(row_tiles):
                nc.tensor.matmul_mx(
                    out=bank[:, a * width : (a + 1) * width],
                    lhsT=w3_loaded[:, FP4_BYTES * a * P : FP4_BYTES * (a + 1) * P].bitcast(FP4X4),
                    lhsT_scale=w3_plane[:, a * P : (a + 1) * P],
                    rhs=codes[:].bitcast(FP8X4),
                    rhs_scale=hid_plane[:],
                    start=True,
                    stop=True,
                )
            result = keep.tile([P, row_tiles * width], F32, name=f"result{c}")
            nc.scalar.copy(out=result[:], in_=bank[:, 0 : row_tiles * width])
            nc.sync.dma_start(out=out_rows[:, :, start : start + width], in_=result[:].rearrange("p (a n) -> p a n", n=width))

        waiting = None
        for c, width in enumerate(PIECES):
            start = sum(PIECES[:c])
            hid = make_hid(c, start, width)
            if waiting is not None:
                finish(*waiting)
            waiting = (c, start, width, hid)
        finish(*waiting)
